import numpy as np
import ml_dtypes


def mxq(x, axis, fmt="e4m3"):
    dtype, down = {"e4m3": (ml_dtypes.float8_e4m3fn, 7), "e5m2": (ml_dtypes.float8_e5m2, 14)}[fmt]
    v = np.moveaxis(np.asarray(x, np.float32).astype(ml_dtypes.bfloat16).astype(np.float64), axis, -1)
    blocks = v.reshape(v.shape[:-1] + (-1, 32))
    amax = np.abs(blocks).max(-1, keepdims=True)
    byte = np.maximum(np.where(amax > 0, np.frexp(amax)[1] - 1 + 127, 0) - down, 1)
    scale = np.exp2(byte - 127.0)
    codes = (blocks / scale).astype(np.float32).astype(dtype).astype(np.float64)
    return np.moveaxis((codes * scale).reshape(v.shape), -1, axis)


WIDE = False


def mx_kscale(k):
    if not WIDE:
        return np.ones(k)
    levels = np.array([30, -30])
    if k % 512:
        return np.exp2(np.random.permutation(np.resize(levels, k // 32))).repeat(32)
    a = np.empty((k // 512, 16))
    for p in range(k // 512):
        a[p, :8] = np.random.permutation(np.resize(levels, 8))
        for g in range(8):
            far = levels[np.abs(levels - a[p, g]) >= 10]
            a[p, g + 8] = far[np.random.randint(len(far))]
    return np.exp2(a.ravel()).repeat(32)


def f64(x):
    return np.asarray(x).astype(np.float64)


def striped(idx):
    return np.tile(np.asarray(idx).reshape(-1, 16).T, (8, 1)).astype(np.uint16)


def unstriped(offs):
    return offs[:16].T.reshape(-1).astype(np.int64)


E2M1 = np.array([0.0, 0.5, 1.0, 1.5, 2.0, 3.0, 4.0, 6.0, -0.0, -0.5, -1.0, -1.5, -2.0, -3.0, -4.0, -6.0])


def pack_weight(w, fmt):
    k, n = w.shape
    w = f64(np.asarray(w, np.float32).astype(ml_dtypes.bfloat16)).reshape(k // 32, 32, n)
    amax = np.abs(w).max(1)
    if fmt in ("e4m3", "e5m2"):
        byte = np.frexp(amax)[1] - 1 + 127 - (7 if fmt == "e4m3" else 14)
    else:
        mant, ex = np.frexp(amax / 6.0)
        byte = np.where(mant > 0.5, ex, ex - 1) + 127
    byte = np.clip(np.where(amax > 0, byte, 1), 1, 254)
    scaled = (w * np.exp2(127.0 - byte)[:, None, :]).reshape(k, n).astype(np.float32)
    by_word = np.ascontiguousarray(scaled.reshape(k // 512, 128, 4, n).transpose(0, 1, 3, 2))
    if fmt in ("e4m3", "e5m2"):
        words = by_word.astype(ml_dtypes.float8_e4m3fn if fmt == "e4m3" else ml_dtypes.float8_e5m2).view(np.uint8)
    else:
        c = by_word.astype(ml_dtypes.float4_e2m1fn).view(np.uint8) & 0xF
        words = (c[..., 0::2] | (c[..., 1::2] << 4)).reshape(k // 512, 128, 2 * n)
    return np.ascontiguousarray(words), np.ascontiguousarray(byte.astype(np.uint8).reshape(k // 512, 16, n))


def unpack_weight(words, scales, fmt):
    g, _, n = scales.shape
    words = np.ascontiguousarray(words).reshape(g, 128, n, -1)
    if fmt in ("e4m3", "e5m2"):
        vals = words.view(ml_dtypes.float8_e4m3fn if fmt == "e4m3" else ml_dtypes.float8_e5m2).astype(np.float64)
    else:
        nib = np.empty((g, 128, n, 4), np.uint8)
        nib[..., 0::2] = words & 0xF
        nib[..., 1::2] = words >> 4
        vals = E2M1[nib]
    vals = vals * np.repeat(np.exp2(scales.astype(np.float64) - 127.0), 8, axis=1)[..., None]
    return vals.transpose(0, 1, 3, 2).reshape(g * 512, n)


K, T, Z, J, R, C, O, Q, N = 512, 1024, 1024, 256, 512, 512, 256, 1024, 256


def setup_inputs():
    n = np.random.standard_normal
    idx = np.random.permutation(T)[:J]
    idx2 = np.random.permutation(Z)[:J]
    idx3 = np.random.permutation(C)[:J]
    idx4 = np.random.permutation(C)[:O]
    idx5 = np.random.permutation(J)[:O]
    idx6 = np.random.permutation(Q)[:O]
    idx7 = np.random.permutation(T)[:O]
    fk = mx_kscale(K)
    fr = mx_kscale(R)
    xtp = pack_weight(n((K, T)) / fk[:, None], "e5m2")
    xop = pack_weight(n((K, Z)) / fk[:, None], "e4m3")
    wp = pack_weight(n((K, R)) * 1 / np.sqrt(K) * fk[:, None] * fr, "e2m1")
    wbp = pack_weight(n((R, N)) * 1 / np.sqrt(R) / fr[:, None], "e2m1")
    wsp = pack_weight(n((K, N)) * 1 / np.sqrt(K) * fk[:, None], "e2m1")
    return {
        "xt_words": xtp[0],
        "xt_scales": xtp[1],
        "xo_words": xop[0],
        "xo_scales": xop[1],
        "w_words": wp[0],
        "w_scales": wp[1],
        "ta": (np.random.uniform(-2.0, 1.0, (R, Q))).astype(np.float32),
        "wb_words": wbp[0],
        "wb_scales": wbp[1],
        "ws_words": wsp[0],
        "ws_scales": wsp[1],
        "offs": striped(idx),
        "offs2": striped(idx2),
        "offs3": striped(idx3),
        "offs4": striped(idx4),
        "offs5": striped(idx5),
        "offs6": striped(idx6),
        "offs7": striped(idx7),
    }


def reference(xt_words, xt_scales, xo_words, xo_scales, w_words, w_scales, ta, wb_words, wb_scales, ws_words, ws_scales, offs, offs2, offs3, offs4, offs5, offs6, offs7):
    idx = unstriped(offs)
    idx2 = unstriped(offs2)
    idx3 = unstriped(offs3)
    idx4 = unstriped(offs4)
    idx5 = unstriped(offs5)
    idx6 = unstriped(offs6)
    idx7 = unstriped(offs7)
    xtu = unpack_weight(xt_words, xt_scales, "e5m2")
    xou = unpack_weight(xo_words, xo_scales, "e4m3")
    wu = unpack_weight(w_words, w_scales, "e2m1")
    wbu = unpack_weight(wb_words, wb_scales, "e2m1")
    wsu = unpack_weight(ws_words, ws_scales, "e2m1")
    xtidxg = xtu[:, idx]
    a = wu.T @ xtidxg
    xoidx2g = xou[:, idx2]
    b = wu.T @ xoidx2g
    pw = np.zeros((R, C))
    pw[:, idx3] = a
    nm = -np.max(f64(ta), axis=1, keepdims=True)
    hid = np.abs(pw[:, idx4] - b[:, idx5]) * np.exp(f64(ta)[:, idx6] + nm)
    hidq = mxq(hid, 0, "e4m3")
    xtidx7g = xtu[:, idx7]
    y = wbu.T @ hidq + wsu.T @ xtidx7g
    return y

@@ -1,0 +1,241 @@
+from contextlib import ExitStack
+
+import concourse.mybir as mybir
+
+K, T, Z, J, R, C, O, Q, N = 512, 1024, 1024, 256, 512, 512, 256, 1024, 256
+FLOPS = 2 * K * R * J * 2 + 2 * R * N * O + 2 * K * N * O
+
+F32 = mybir.dt.float32
+BF16 = mybir.dt.bfloat16
+I32 = mybir.dt.int32
+U32 = mybir.dt.uint32
+U16 = mybir.dt.uint16
+U8 = mybir.dt.uint8
+E4M3 = mybir.dt.float8_e4m3fn_x4
+E5M2 = mybir.dt.float8_e5m2_x4
+E2M1 = mybir.dt.float4_e2m1fn_x4
+ACT = mybir.ActivationFunctionType
+ALU = mybir.AluOpType
+AX = mybir.AxisListType
+
+P = 128
+PACK = 4
+QUADS = 4
+HALF = O // 2
+
+
+def tile_list_fadedread_oneforboth_further_plain_kernel(
+    tc, xt_words, xt_scales, xo_words, xo_scales, w_words, w_scales, ta, wb_words, wb_scales,
+    ws_words, ws_scales, offs, offs2, offs3, offs4, offs5, offs6, offs7, out,
+):
+    nc = tc.nc
+    with ExitStack() as ctx:
+        sb = ctx.enter_context(tc.tile_pool(name="sb", bufs=1))
+        ps = ctx.enter_context(tc.psum_pool(name="ps", bufs=1))
+
+        def tile(name, shape, dtype):
+            return sb.tile(shape, dtype, name=name, align_bytes=64)
+
+        def load_list(name, src):
+            lst = sb.tile([P, src.shape[1]], U16, name=name)
+            nc.sync.dma_start(lst[:], src)
+            return lst
+
+        def zero_plane(name, width):
+            plane = tile(name, [P, width], U8)
+            nc.vector.memset(plane[:].bitcast(I32), 0)
+            return plane
+
+        def load_scale_rows(plane, src):
+            rows = src[0].bitcast(I32)
+            for q in range(QUADS):
+                nc.sync.dma_start(plane[32 * q : 32 * q + 4, :].bitcast(I32), rows[4 * q : 4 * q + 4, :])
+
+        def load_words8(name, src, queue):
+            words = tile(name, [P, src.shape[2]], I32)
+            queue.dma_start(words[:], src[0].rearrange("p n t -> p (n t)").bitcast(I32))
+            return words
+
+        def load_words4(name, src):
+            words = tile(name, [P, src.shape[2]], U8)
+            nc.sync.dma_start(words[:].bitcast(I32), src[0].bitcast(I32))
+            return words
+
+        def gather_packed(name, words, plane, lst):
+            gw = tile(name + "_w", [P, J], U32)
+            gs = tile(name + "_s", [P, J], U8)
+            nc.vector.tensor_copy(gw[:], words[:].bitcast(U32).indirect(lst[:]))
+            nc.vector.tensor_copy(gs[:], plane[:].indirect(lst[:]))
+            return gw, gs
+
+        w_rows = tile("w_rows", [P, QUADS * R], U8)
+        xt_plane = zero_plane("xt_plane", T)
+        w_plane = zero_plane("w_plane", R)
+        xo_plane = zero_plane("xo_plane", Z)
+        pw = [tile("pw%d" % t, [P, C], F32) for t in range(PACK)]
+        for t in range(PACK):
+            nc.vector.memset(pw[t][:], 0.0)
+        b_sb = tile("b_sb", [P, (PACK + 1) * J], F32)
+        nc.vector.memset(b_sb[:, PACK * J :], 0.0)
+        ws_plane = zero_plane("ws_plane", N)
+        wb_plane = zero_plane("wb_plane", N)
+
+        xt_w = load_words8("xt_w", xt_words, nc.scalar)
+        w_w = load_words4("w_w", w_words)
+        l1 = load_list("l1", offs)
+        nc.sync.dma_start(
+            w_rows[0:4, :].bitcast(I32).rearrange("r (q c) -> r q c", q=QUADS),
+            w_scales[0].bitcast(I32).rearrange("(q r) c -> r q c", q=QUADS),
+        )
+        load_scale_rows(xt_plane, xt_scales)
+        xo_w = load_words8("xo_w", xo_words, nc.sync)
+        l2 = load_list("l2", offs2)
+        load_scale_rows(xo_plane, xo_scales)
+        l3 = load_list("l3", offs3)
+        ta_rows = ta.rearrange("(p t) q -> p t q", t=PACK)
+        ta_sb = [tile("ta%d" % t, [P, Q], F32) for t in range(PACK)]
+        nc.sync.dma_start(ta_sb[0][:], ta_rows[:, 0, :])
+        nc.sync.dma_start(ta_sb[1][:], ta_rows[:, 1, :])
+        l5 = load_list("l5", offs5)
+        l6 = load_list("l6", offs6)
+        nc.sync.dma_start(ta_sb[2][:], ta_rows[:, 2, :])
+        nc.sync.dma_start(ta_sb[3][:], ta_rows[:, 3, :])
+        l4 = load_list("l4", offs4)
+        l7 = load_list("l7", offs7)
+        ws_w = load_words4("ws_w", ws_words)
+        load_scale_rows(ws_plane, ws_scales)
+        wb_w = load_words4("wb_w", wb_words)
+        load_scale_rows(wb_plane, wb_scales)
+
+        wp_w = tile("wp_w", [P, 2 * R], U8)
+        nc.vector.tensor_copy(
+            wp_w[:].bitcast(U16).rearrange("p (t m) -> p t m", t=PACK),
+            w_w[:].bitcast(U16).rearrange("p (m t) -> p t m", t=PACK),
+        )
+        for q in range(QUADS):
+            nc.vector.tensor_copy(
+                w_plane[32 * q : 32 * q + 4, :].bitcast(I32),
+                w_rows[0:4, q * R : (q + 1) * R].bitcast(I32),
+            )
+        wp_s = tile("wp_s", [P, R], U8)
+        nc.vector.tensor_copy(
+            wp_s[:].rearrange("p (t m) -> p t m", t=PACK),
+            w_plane[:].rearrange("p (m t) -> p t m", t=PACK),
+        )
+
+        def first_stage(name, gw, gs, fmt):
+            banks = [ps.tile([P, 2 * J], F32, name="%s%d" % (name, u)) for u in range(2)]
+            for t in range(PACK):
+                nc.tensor.matmul_mx(
+                    out=banks[t // 2][:, (t % 2) * J : (t % 2 + 1) * J],
+                    lhsT=wp_w[:, 2 * P * t : 2 * P * (t + 1)].bitcast(E2M1),
+                    lhsT_scale=wp_s[:, P * t : P * (t + 1)],
+                    rhs=gw[:].bitcast(fmt),
+                    rhs_scale=gs[:],
+                    start=True,
+                    stop=True,
+                )
+            return banks
+
+        g1w, g1s = gather_packed("g1", xt_w, xt_plane, l1)
+        a_ps = first_stage("a_ps", g1w, g1s, E5M2)
+        g2w, g2s = gather_packed("g2", xo_w, xo_plane, l2)
+        b_ps = first_stage("b_ps", g2w, g2s, E4M3)
+
+        a_sb = [tile("a_sb%d" % u, [P, 2 * J], F32) for u in range(2)]
+        nm = [tile("nm%d" % t, [P, 1], F32) for t in range(PACK)]
+        ex = tile("ex", [P, PACK, O], F32)
+        bg = tile("bg", [P, PACK, O], F32)
+        df = tile("df", [P, PACK, O], F32)
+        m0 = tile("m0", [P, PACK, HALF], F32)
+        m1 = tile("m1", [P, PACK, HALF], F32)
+
+        def a_of(t):
+            return a_sb[t // 2][:, (t % 2) * J : (t % 2 + 1) * J]
+
+        def scatter_scalar(t):
+            nc.scalar.activation(out=pw[t][:].indirect(l3[:]), in_=a_of(t), func=ACT.Copy)
+
+        def scatter_vector(t):
+            nc.vector.tensor_copy(pw[t][:].indirect(l3[:]), a_of(t))
+
+        def row_max(t):
+            nc.vector.tensor_reduce(out=nm[t][:], in_=ta_sb[t][:], axis=AX.X, op=ALU.max, negate=True)
+
+        def look_b(t):
+            nc.scalar.activation(
+                out=bg[:, t, :], in_=b_sb[:, t * J : (t + 2) * J].indirect(l5[:]), func=ACT.Copy
+            )
+
+        def look_exp(t):
+            nc.scalar.activation(out=ex[:, t, :], in_=ta_sb[t][:].indirect(l6[:]), func=ACT.Exp, bias=nm[t][:])
+
+        def diff(t):
+            nc.vector.tensor_tensor(df[:, t, :], pw[t][:].indirect(l4[:]), bg[:, t, :], ALU.subtract)
+
+        def scale(t):
+            nc.vector.tensor_tensor(m0[:, t, :], df[:, t, 0:HALF], ex[:, t, 0:HALF], ALU.mult)
+            nc.scalar.activation(out=m1[:, t, :], in_=df[:, t, HALF:O], func=ACT.Abs)
+
+        nc.scalar.copy(a_sb[0][:], a_ps[0][:])
+        nc.scalar.copy(a_sb[1][:], a_ps[1][:])
+        scatter_scalar(0)
+        row_max(0)
+        scatter_vector(3)
+        nc.scalar.copy(b_sb[:, 0 : 2 * J], b_ps[0][:])
+        nc.scalar.copy(b_sb[:, 2 * J : 4 * J], b_ps[1][:])
+        scatter_scalar(1)
+        row_max(1)
+        row_max(2)
+        row_max(3)
+        scatter_scalar(2)
+        g7w, g7s = gather_packed("g7", xt_w, xt_plane, l7)
+        y_ps = [[ps.tile([P, HALF], F32, name="y%d%d" % (h, n)) for n in range(2)] for h in range(2)]
+        for h in range(2):
+            for n in range(2):
+                nc.tensor.matmul_mx(
+                    out=y_ps[h][n][:],
+                    lhsT=ws_w[:, 2 * P * n : 2 * P * (n + 1)].bitcast(E2M1),
+                    lhsT_scale=ws_plane[:, P * n : P * (n + 1)],
+                    rhs=g7w[:, h * HALF : (h + 1) * HALF].bitcast(E5M2),
+                    rhs_scale=g7s[:, h * HALF : (h + 1) * HALF],
+                    start=True,
+                    stop=False,
+                )
+        for t in range(PACK):
+            look_b(t)
+        for t in range(PACK):
+            diff(t)
+            look_exp(t)
+            scale(t)
+
+        hb = [tile("hb%d" % h, [P, HALF * PACK], BF16) for h in range(2)]
+
+        def woven(h):
+            return hb[h][:].rearrange("p (c i t) -> p c t i", i=4, t=PACK)
+
+        def planes(src):
+            return src.rearrange("p t (c i) -> p c t i", i=4)
+
+        nc.scalar.activation(out=woven(0), in_=planes(m0[:]), func=ACT.Abs)
+        nc.vector.tensor_tensor(woven(1), planes(m1[:]), planes(ex[:, :, HALF:O]), ALU.mult)
+
+        out_rows = out.rearrange("(n p) o -> p n o", p=P)
+        for h in (1, 0):
+            hq = tile("hq%d" % h, [P, HALF], U32)
+            hs = tile("hs%d" % h, [P, HALF], U8)
+            nc.vector.quantize_mx(out=hq[:].bitcast(E4M3), scales=hs[:], in_=hb[h][:])
+            y_sb = tile("y_sb%d" % h, [P, 2, HALF], F32)
+            for n in range(2):
+                nc.tensor.matmul_mx(
+                    out=y_ps[h][n][:],
+                    lhsT=wb_w[:, 2 * P * n : 2 * P * (n + 1)].bitcast(E2M1),
+                    lhsT_scale=wb_plane[:, P * n : P * (n + 1)],
+                    rhs=hq[:].bitcast(E4M3),
+                    rhs_scale=hs[:],
+                    start=False,
+                    stop=True,
+                )
+            nc.scalar.copy(y_sb[:, 0, :], y_ps[h][0][:])
+            nc.vector.tensor_copy(y_sb[:, 1, :], y_ps[h][1][:])
+            nc.sync.dma_start(out_rows[:, :, h * HALF : (h + 1) * HALF], y_sb[:])

@@ -33,17 +33,17 @@ def tile_list_fadedread_oneforboth_further_plain_kernel(
         sb = ctx.enter_context(tc.tile_pool(name="sb", bufs=1))
         ps = ctx.enter_context(tc.psum_pool(name="ps", bufs=1))
 
-        def tile(name, shape, dtype):
-            return sb.tile(shape, dtype, name=name, align_bytes=64)
+        def tile(name, shape, dtype, tag=None):
+            return sb.tile(shape, dtype, name=name, tag=tag or name, align_bytes=64)
 
         def load_list(name, src):
             lst = sb.tile([P, src.shape[1]], U16, name=name)
             nc.sync.dma_start(lst[:], src)
             return lst
 
-        def zero_plane(name, width):
+        def zero_plane(name, width, engine):
             plane = tile(name, [P, width], U8)
-            nc.vector.memset(plane[:].bitcast(I32), 0)
+            engine.memset(plane[:].bitcast(I32), 0)
             return plane
 
         def load_scale_rows(plane, src):
@@ -64,42 +64,39 @@ def tile_list_fadedread_oneforboth_further_plain_kernel(
         def gather_packed(name, words, plane, lst):
             gw = tile(name + "_w", [P, J], U32)
             gs = tile(name + "_s", [P, J], U8)
-            nc.vector.tensor_copy(gw[:], words[:].bitcast(U32).indirect(lst[:]))
             nc.vector.tensor_copy(gs[:], plane[:].indirect(lst[:]))
+            nc.vector.tensor_copy(gw[:], words[:].bitcast(U32).indirect(lst[:]))
             return gw, gs
 
         w_rows = tile("w_rows", [P, QUADS * R], U8)
-        xt_plane = zero_plane("xt_plane", T)
-        w_plane = zero_plane("w_plane", R)
-        xo_plane = zero_plane("xo_plane", Z)
-        pw = [tile("pw%d" % t, [P, C], F32) for t in range(PACK)]
-        for t in range(PACK):
-            nc.vector.memset(pw[t][:], 0.0)
+        xt_plane = zero_plane("xt_plane", T, nc.vector)
+        w_plane = zero_plane("w_plane", R, nc.vector)
+        xo_plane = zero_plane("xo_plane", Z, nc.vector)
+        ws_plane = zero_plane("ws_plane", N, nc.gpsimd)
+        wb_plane = zero_plane("wb_plane", N, nc.gpsimd)
         b_sb = tile("b_sb", [P, (PACK + 1) * J], F32)
-        nc.vector.memset(b_sb[:, PACK * J :], 0.0)
-        ws_plane = zero_plane("ws_plane", N)
-        wb_plane = zero_plane("wb_plane", N)
+        nc.gpsimd.memset(b_sb[:, PACK * J :], 0.0)
+        pw = [tile("pw%d" % t, [P, C], F32) for t in range(PACK)]
+        nc.gpsimd.memset(pw[2][:], 0.0)
 
-        xt_w = load_words8("xt_w", xt_words, nc.scalar)
-        w_w = load_words4("w_w", w_words)
-        l1 = load_list("l1", offs)
         nc.sync.dma_start(
             w_rows[0:4, :].bitcast(I32).rearrange("r (q c) -> r q c", q=QUADS),
             w_scales[0].bitcast(I32).rearrange("(q r) c -> r q c", q=QUADS),
         )
+        l1 = load_list("l1", offs)
+        w_w = load_words4("w_w", w_words)
         load_scale_rows(xt_plane, xt_scales)
-        xo_w = load_words8("xo_w", xo_words, nc.sync)
-        l2 = load_list("l2", offs2)
+        xt_w = load_words8("xt_w", xt_words, nc.sync)
         load_scale_rows(xo_plane, xo_scales)
+        l2 = load_list("l2", offs2)
+        xo_w = load_words8("xo_w", xo_words, nc.sync)
         l3 = load_list("l3", offs3)
         ta_rows = ta.rearrange("(p t) q -> p t q", t=PACK)
         ta_sb = [tile("ta%d" % t, [P, Q], F32) for t in range(PACK)]
-        nc.sync.dma_start(ta_sb[0][:], ta_rows[:, 0, :])
-        nc.sync.dma_start(ta_sb[1][:], ta_rows[:, 1, :])
+        for t in range(PACK):
+            nc.sync.dma_start(ta_sb[t][:], ta_rows[:, t, :])
         l5 = load_list("l5", offs5)
         l6 = load_list("l6", offs6)
-        nc.sync.dma_start(ta_sb[2][:], ta_rows[:, 2, :])
-        nc.sync.dma_start(ta_sb[3][:], ta_rows[:, 3, :])
         l4 = load_list("l4", offs4)
         l7 = load_list("l7", offs7)
         ws_w = load_words4("ws_w", ws_words)
@@ -108,7 +105,7 @@ def tile_list_fadedread_oneforboth_further_plain_kernel(
         load_scale_rows(wb_plane, wb_scales)
 
         wp_w = tile("wp_w", [P, 2 * R], U8)
-        nc.vector.tensor_copy(
+        nc.scalar.copy(
             wp_w[:].bitcast(U16).rearrange("p (t m) -> p t m", t=PACK),
             w_w[:].bitcast(U16).rearrange("p (m t) -> p t m", t=PACK),
         )
@@ -142,11 +139,11 @@ def tile_list_fadedread_oneforboth_further_plain_kernel(
         g2w, g2s = gather_packed("g2", xo_w, xo_plane, l2)
         b_ps = first_stage("b_ps", g2w, g2s, E4M3)
 
+        for t in (0, 3, 1):
+            nc.vector.memset(pw[t][:], 0.0)
         a_sb = [tile("a_sb%d" % u, [P, 2 * J], F32) for u in range(2)]
         nm = [tile("nm%d" % t, [P, 1], F32) for t in range(PACK)]
-        ex = tile("ex", [P, PACK, O], F32)
         bg = tile("bg", [P, PACK, O], F32)
-        df = tile("df", [P, PACK, O], F32)
         m0 = tile("m0", [P, PACK, HALF], F32)
         m1 = tile("m1", [P, PACK, HALF], F32)
 
@@ -163,9 +160,11 @@ def tile_list_fadedread_oneforboth_further_plain_kernel(
             nc.vector.tensor_reduce(out=nm[t][:], in_=ta_sb[t][:], axis=AX.X, op=ALU.max, negate=True)
 
         def look_b(t):
-            nc.scalar.activation(
-                out=bg[:, t, :], in_=b_sb[:, t * J : (t + 2) * J].indirect(l5[:]), func=ACT.Copy
-            )
+            window = b_sb[:, t * J : (t + 2) * J].indirect(l5[:])
+            if t < 2:
+                nc.scalar.activation(out=bg[:, t, :], in_=window, func=ACT.Copy)
+            else:
+                nc.vector.tensor_copy(bg[:, t, :], window)
 
         def look_exp(t):
             nc.scalar.activation(out=ex[:, t, :], in_=ta_sb[t][:].indirect(l6[:]), func=ACT.Exp, bias=nm[t][:])
@@ -204,7 +203,9 @@ def tile_list_fadedread_oneforboth_further_plain_kernel(
                 )
         for t in range(PACK):
             look_b(t)
-        for t in range(PACK):
+        df = tile("df", [P, PACK, O], F32, tag="xt_w")
+        ex = tile("ex", [P, PACK, O], F32, tag="b_sb")
+        for t in (3, 0, 1, 2):
             diff(t)
             look_exp(t)
             scale(t)

@@ -87,9 +87,10 @@ def tile_list_fadedread_oneforboth_further_plain_kernel(
         w_w = load_words4("w_w", w_words)
         load_scale_rows(xt_plane, xt_scales)
         xt_w = load_words8("xt_w", xt_words, nc.sync)
-        load_scale_rows(xo_plane, xo_scales)
-        l2 = load_list("l2", offs2)
+        l7 = load_list("l7", offs7)
         xo_w = load_words8("xo_w", xo_words, nc.sync)
+        l2 = load_list("l2", offs2)
+        load_scale_rows(xo_plane, xo_scales)
         l3 = load_list("l3", offs3)
         ta_rows = ta.rearrange("(p t) q -> p t q", t=PACK)
         ta_sb = [tile("ta%d" % t, [P, Q], F32) for t in range(PACK)]
@@ -98,7 +99,6 @@ def tile_list_fadedread_oneforboth_further_plain_kernel(
         l5 = load_list("l5", offs5)
         l6 = load_list("l6", offs6)
         l4 = load_list("l4", offs4)
-        l7 = load_list("l7", offs7)
         ws_w = load_words4("ws_w", ws_words)
         load_scale_rows(ws_plane, ws_scales)
         wb_w = load_words4("wb_w", wb_words)
@@ -136,6 +136,7 @@ def tile_list_fadedread_oneforboth_further_plain_kernel(
 
         g1w, g1s = gather_packed("g1", xt_w, xt_plane, l1)
         a_ps = first_stage("a_ps", g1w, g1s, E5M2)
+        g7w, g7s = gather_packed("g7", xt_w, xt_plane, l7)
         g2w, g2s = gather_packed("g2", xo_w, xo_plane, l2)
         b_ps = first_stage("b_ps", g2w, g2s, E4M3)
 
@@ -161,7 +162,7 @@ def tile_list_fadedread_oneforboth_further_plain_kernel(
 
         def look_b(t):
             window = b_sb[:, t * J : (t + 2) * J].indirect(l5[:])
-            if t < 2:
+            if t < 3:
                 nc.scalar.activation(out=bg[:, t, :], in_=window, func=ACT.Copy)
             else:
                 nc.vector.tensor_copy(bg[:, t, :], window)
@@ -171,10 +172,6 @@ def tile_list_fadedread_oneforboth_further_plain_kernel(
 
         def diff(t):
             nc.vector.tensor_tensor(df[:, t, :], pw[t][:].indirect(l4[:]), bg[:, t, :], ALU.subtract)
-
-        def scale(t):
-            nc.vector.tensor_tensor(m0[:, t, :], df[:, t, 0:HALF], ex[:, t, 0:HALF], ALU.mult)
-            nc.scalar.activation(out=m1[:, t, :], in_=df[:, t, HALF:O], func=ACT.Abs)
 
         nc.scalar.copy(a_sb[0][:], a_ps[0][:])
         nc.scalar.copy(a_sb[1][:], a_ps[1][:])
@@ -188,7 +185,6 @@ def tile_list_fadedread_oneforboth_further_plain_kernel(
         row_max(2)
         row_max(3)
         scatter_scalar(2)
-        g7w, g7s = gather_packed("g7", xt_w, xt_plane, l7)
         y_ps = [[ps.tile([P, HALF], F32, name="y%d%d" % (h, n)) for n in range(2)] for h in range(2)]
         for h in range(2):
             for n in range(2):
@@ -203,12 +199,13 @@ def tile_list_fadedread_oneforboth_further_plain_kernel(
                 )
         for t in range(PACK):
             look_b(t)
-        df = tile("df", [P, PACK, O], F32, tag="xt_w")
+        df = tile("df", [P, PACK, O], F32)
         ex = tile("ex", [P, PACK, O], F32, tag="b_sb")
-        for t in (3, 0, 1, 2):
+        for t in range(PACK):
             diff(t)
             look_exp(t)
-            scale(t)
+        nc.vector.tensor_tensor(m0[:], df[:, :, 0:HALF], ex[:, :, 0:HALF], ALU.mult)
+        nc.scalar.activation(out=m1[:], in_=df[:, :, HALF:O], func=ACT.Abs)
 
         hb = [tile("hb%d" % h, [P, HALF * PACK], BF16) for h in range(2)]
 

@@ -115,10 +115,14 @@ def tile_list_fadedread_oneforboth_further_plain_kernel(
                 w_rows[0:4, q * R : (q + 1) * R].bitcast(I32),
             )
         wp_s = tile("wp_s", [P, R], U8)
-        nc.vector.tensor_copy(
-            wp_s[:].rearrange("p (t m) -> p t m", t=PACK),
-            w_plane[:].rearrange("p (m t) -> p t m", t=PACK),
-        )
+
+        def deal_scales(t0):
+            nc.vector.tensor_copy(
+                wp_s[:].rearrange("p (t m) -> p t m", t=PACK)[:, t0 : t0 + 2, :],
+                w_plane[:].rearrange("p (m t) -> p t m", t=PACK)[:, t0 : t0 + 2, :],
+            )
+
+        deal_scales(0)
 
         def first_stage(name, gw, gs, fmt):
             banks = [ps.tile([P, 2 * J], F32, name="%s%d" % (name, u)) for u in range(2)]
@@ -135,6 +139,7 @@ def tile_list_fadedread_oneforboth_further_plain_kernel(
             return banks
 
         g1w, g1s = gather_packed("g1", xt_w, xt_plane, l1)
+        deal_scales(2)
         a_ps = first_stage("a_ps", g1w, g1s, E5M2)
         g7w, g7s = gather_packed("g7", xt_w, xt_plane, l7)
         g2w, g2s = gather_packed("g2", xo_w, xo_plane, l2)
@@ -162,7 +167,7 @@ def tile_list_fadedread_oneforboth_further_plain_kernel(
 
         def look_b(t):
             window = b_sb[:, t * J : (t + 2) * J].indirect(l5[:])
-            if t < 3:
+            if t < 2:
                 nc.scalar.activation(out=bg[:, t, :], in_=window, func=ACT.Copy)
             else:
                 nc.vector.tensor_copy(bg[:, t, :], window)
@@ -204,8 +209,10 @@ def tile_list_fadedread_oneforboth_further_plain_kernel(
         for t in range(PACK):
             diff(t)
             look_exp(t)
-        nc.vector.tensor_tensor(m0[:], df[:, :, 0:HALF], ex[:, :, 0:HALF], ALU.mult)
-        nc.scalar.activation(out=m1[:], in_=df[:, :, HALF:O], func=ACT.Abs)
+            if t >= PACK - 2:
+                ts = slice(0, PACK - 1) if t == PACK - 2 else slice(PACK - 1, PACK)
+                nc.vector.tensor_tensor(m0[:, ts, :], df[:, ts, 0:HALF], ex[:, ts, 0:HALF], ALU.mult)
+                nc.scalar.activation(out=m1[:, ts, :], in_=df[:, ts, HALF:O], func=ACT.Abs)
 
         hb = [tile("hb%d" % h, [P, HALF * PACK], BF16) for h in range(2)]
 

from contextlib import ExitStack

import concourse.mybir as mybir

K, T, Z, J, R, C, O, Q, N = 512, 1024, 1024, 256, 512, 512, 256, 1024, 256
FLOPS = 2 * K * R * J * 2 + 2 * R * N * O + 2 * K * N * O

F32 = mybir.dt.float32
BF16 = mybir.dt.bfloat16
I32 = mybir.dt.int32
U32 = mybir.dt.uint32
U16 = mybir.dt.uint16
U8 = mybir.dt.uint8
E4M3 = mybir.dt.float8_e4m3fn_x4
E5M2 = mybir.dt.float8_e5m2_x4
E2M1 = mybir.dt.float4_e2m1fn_x4
ACT = mybir.ActivationFunctionType
ALU = mybir.AluOpType
AX = mybir.AxisListType

P = 128
PACK = 4
QUADS = 4
HALF = O // 2


def tile_list_fadedread_oneforboth_further_plain_kernel(
    tc, xt_words, xt_scales, xo_words, xo_scales, w_words, w_scales, ta, wb_words, wb_scales,
    ws_words, ws_scales, offs, offs2, offs3, offs4, offs5, offs6, offs7, out,
):
    nc = tc.nc
    with ExitStack() as ctx:
        sb = ctx.enter_context(tc.tile_pool(name="sb", bufs=1))
        ps = ctx.enter_context(tc.psum_pool(name="ps", bufs=1))

        def tile(name, shape, dtype, tag=None):
            return sb.tile(shape, dtype, name=name, tag=tag or name, align_bytes=64)

        def load_list(name, src):
            lst = sb.tile([P, src.shape[1]], U16, name=name)
            nc.sync.dma_start(lst[:], src)
            return lst

        def zero_plane(name, width, engine):
            plane = tile(name, [P, width], U8)
            engine.memset(plane[:].bitcast(I32), 0)
            return plane

        def load_scale_rows(plane, src):
            rows = src[0].bitcast(I32)
            for q in range(QUADS):
                nc.sync.dma_start(plane[32 * q : 32 * q + 4, :].bitcast(I32), rows[4 * q : 4 * q + 4, :])

        def load_words8(name, src, queue):
            words = tile(name, [P, src.shape[2]], I32)
            queue.dma_start(words[:], src[0].rearrange("p n t -> p (n t)").bitcast(I32))
            return words

        def load_words4(name, src):
            words = tile(name, [P, src.shape[2]], U8)
            nc.sync.dma_start(words[:].bitcast(I32), src[0].bitcast(I32))
            return words

        def gather_packed(name, words, plane, lst):
            gw = tile(name + "_w", [P, J], U32)
            gs = tile(name + "_s", [P, J], U8)
            nc.vector.tensor_copy(gs[:], plane[:].indirect(lst[:]))
            nc.vector.tensor_copy(gw[:], words[:].bitcast(U32).indirect(lst[:]))
            return gw, gs

        w_rows = tile("w_rows", [P, QUADS * R], U8)
        xt_plane = zero_plane("xt_plane", T, nc.vector)
        w_plane = zero_plane("w_plane", R, nc.vector)
        xo_plane = zero_plane("xo_plane", Z, nc.vector)
        ws_plane = zero_plane("ws_plane", N, nc.gpsimd)
        wb_plane = zero_plane("wb_plane", N, nc.gpsimd)
        b_sb = tile("b_sb", [P, (PACK + 1) * J], F32)
        nc.gpsimd.memset(b_sb[:, PACK * J :], 0.0)
        pw = [tile("pw%d" % t, [P, C], F32) for t in range(PACK)]
        nc.gpsimd.memset(pw[2][:], 0.0)

        nc.sync.dma_start(
            w_rows[0:4, :].bitcast(I32).rearrange("r (q c) -> r q c", q=QUADS),
            w_scales[0].bitcast(I32).rearrange("(q r) c -> r q c", q=QUADS),
        )
        l1 = load_list("l1", offs)
        w_w = load_words4("w_w", w_words)
        load_scale_rows(xt_plane, xt_scales)
        xt_w = load_words8("xt_w", xt_words, nc.sync)
        l7 = load_list("l7", offs7)
        xo_w = load_words8("xo_w", xo_words, nc.sync)
        l2 = load_list("l2", offs2)
        load_scale_rows(xo_plane, xo_scales)
        l3 = load_list("l3", offs3)
        ta_rows = ta.rearrange("(p t) q -> p t q", t=PACK)
        ta_sb = [tile("ta%d" % t, [P, Q], F32) for t in range(PACK)]
        for t in range(PACK):
            nc.sync.dma_start(ta_sb[t][:], ta_rows[:, t, :])
        l5 = load_list("l5", offs5)
        l6 = load_list("l6", offs6)
        l4 = load_list("l4", offs4)
        ws_w = load_words4("ws_w", ws_words)
        load_scale_rows(ws_plane, ws_scales)
        wb_w = load_words4("wb_w", wb_words)
        load_scale_rows(wb_plane, wb_scales)

        wp_w = tile("wp_w", [P, 2 * R], U8)
        nc.scalar.copy(
            wp_w[:].bitcast(U16).rearrange("p (t m) -> p t m", t=PACK),
            w_w[:].bitcast(U16).rearrange("p (m t) -> p t m", t=PACK),
        )
        for q in range(QUADS):
            nc.vector.tensor_copy(
                w_plane[32 * q : 32 * q + 4, :].bitcast(I32),
                w_rows[0:4, q * R : (q + 1) * R].bitcast(I32),
            )
        wp_s = tile("wp_s", [P, R], U8)

        def deal_scales(t0):
            nc.vector.tensor_copy(
                wp_s[:].rearrange("p (t m) -> p t m", t=PACK)[:, t0 : t0 + 2, :],
                w_plane[:].rearrange("p (m t) -> p t m", t=PACK)[:, t0 : t0 + 2, :],
            )

        deal_scales(0)

        def first_stage(name, gw, gs, fmt):
            banks = [ps.tile([P, 2 * J], F32, name="%s%d" % (name, u)) for u in range(2)]
            for t in range(PACK):
                nc.tensor.matmul_mx(
                    out=banks[t // 2][:, (t % 2) * J : (t % 2 + 1) * J],
                    lhsT=wp_w[:, 2 * P * t : 2 * P * (t + 1)].bitcast(E2M1),
                    lhsT_scale=wp_s[:, P * t : P * (t + 1)],
                    rhs=gw[:].bitcast(fmt),
                    rhs_scale=gs[:],
                    start=True,
                    stop=True,
                )
            return banks

        g1w, g1s = gather_packed("g1", xt_w, xt_plane, l1)
        deal_scales(2)
        a_ps = first_stage("a_ps", g1w, g1s, E5M2)
        g7w, g7s = gather_packed("g7", xt_w, xt_plane, l7)
        g2w, g2s = gather_packed("g2", xo_w, xo_plane, l2)
        b_ps = first_stage("b_ps", g2w, g2s, E4M3)

        for t in (0, 3, 1):
            nc.vector.memset(pw[t][:], 0.0)
        a_sb = [tile("a_sb%d" % u, [P, 2 * J], F32) for u in range(2)]
        nm = [tile("nm%d" % t, [P, 1], F32) for t in range(PACK)]
        bg = tile("bg", [P, PACK, O], F32)
        m0 = tile("m0", [P, PACK, HALF], F32)
        m1 = tile("m1", [P, PACK, HALF], F32)

        def a_of(t):
            return a_sb[t // 2][:, (t % 2) * J : (t % 2 + 1) * J]

        def scatter_scalar(t):
            nc.scalar.activation(out=pw[t][:].indirect(l3[:]), in_=a_of(t), func=ACT.Copy)

        def scatter_vector(t):
            nc.vector.tensor_copy(pw[t][:].indirect(l3[:]), a_of(t))

        def row_max(t):
            nc.vector.tensor_reduce(out=nm[t][:], in_=ta_sb[t][:], axis=AX.X, op=ALU.max, negate=True)

        def look_b(t):
            window = b_sb[:, t * J : (t + 2) * J].indirect(l5[:])
            if t < 2:
                nc.scalar.activation(out=bg[:, t, :], in_=window, func=ACT.Copy)
            else:
                nc.vector.tensor_copy(bg[:, t, :], window)

        def look_exp(t):
            nc.scalar.activation(out=ex[:, t, :], in_=ta_sb[t][:].indirect(l6[:]), func=ACT.Exp, bias=nm[t][:])

        def diff(t):
            nc.vector.tensor_tensor(df[:, t, :], pw[t][:].indirect(l4[:]), bg[:, t, :], ALU.subtract)

        nc.scalar.copy(a_sb[0][:], a_ps[0][:])
        nc.scalar.copy(a_sb[1][:], a_ps[1][:])
        scatter_scalar(0)
        row_max(0)
        scatter_vector(3)
        nc.scalar.copy(b_sb[:, 0 : 2 * J], b_ps[0][:])
        nc.scalar.copy(b_sb[:, 2 * J : 4 * J], b_ps[1][:])
        scatter_scalar(1)
        row_max(1)
        row_max(2)
        row_max(3)
        scatter_scalar(2)
        y_ps = [[ps.tile([P, HALF], F32, name="y%d%d" % (h, n)) for n in range(2)] for h in range(2)]
        for h in range(2):
            for n in range(2):
                nc.tensor.matmul_mx(
                    out=y_ps[h][n][:],
                    lhsT=ws_w[:, 2 * P * n : 2 * P * (n + 1)].bitcast(E2M1),
                    lhsT_scale=ws_plane[:, P * n : P * (n + 1)],
                    rhs=g7w[:, h * HALF : (h + 1) * HALF].bitcast(E5M2),
                    rhs_scale=g7s[:, h * HALF : (h + 1) * HALF],
                    start=True,
                    stop=False,
                )
        for t in range(PACK):
            look_b(t)
        df = tile("df", [P, PACK, O], F32)
        ex = tile("ex", [P, PACK, O], F32, tag="b_sb")
        for t in range(PACK):
            diff(t)
            look_exp(t)
            if t >= PACK - 2:
                ts = slice(0, PACK - 1) if t == PACK - 2 else slice(PACK - 1, PACK)
                nc.vector.tensor_tensor(m0[:, ts, :], df[:, ts, 0:HALF], ex[:, ts, 0:HALF], ALU.mult)
                nc.scalar.activation(out=m1[:, ts, :], in_=df[:, ts, HALF:O], func=ACT.Abs)

        hb = [tile("hb%d" % h, [P, HALF * PACK], BF16) for h in range(2)]

        def woven(h):
            return hb[h][:].rearrange("p (c i t) -> p c t i", i=4, t=PACK)

        def planes(src):
            return src.rearrange("p t (c i) -> p c t i", i=4)

        nc.scalar.activation(out=woven(0), in_=planes(m0[:]), func=ACT.Abs)
        nc.vector.tensor_tensor(woven(1), planes(m1[:]), planes(ex[:, :, HALF:O]), ALU.mult)

        out_rows = out.rearrange("(n p) o -> p n o", p=P)
        for h in (1, 0):
            hq = tile("hq%d" % h, [P, HALF], U32)
            hs = tile("hs%d" % h, [P, HALF], U8)
            nc.vector.quantize_mx(out=hq[:].bitcast(E4M3), scales=hs[:], in_=hb[h][:])
            y_sb = tile("y_sb%d" % h, [P, 2, HALF], F32)
            for n in range(2):
                nc.tensor.matmul_mx(
                    out=y_ps[h][n][:],
                    lhsT=wb_w[:, 2 * P * n : 2 * P * (n + 1)].bitcast(E2M1),
                    lhsT_scale=wb_plane[:, P * n : P * (n + 1)],
                    rhs=hq[:].bitcast(E4M3),
                    rhs_scale=hs[:],
                    start=False,
                    stop=True,
                )
            nc.scalar.copy(y_sb[:, 0, :], y_ps[h][0][:])
            nc.vector.tensor_copy(y_sb[:, 1, :], y_ps[h][1][:])
            nc.sync.dma_start(out_rows[:, :, h * HALF : (h + 1) * HALF], y_sb[:])
